import numpy as np
CORES = [33,34,161,162,289,290,417,418]
N = 8
J, Q = 256, 1024
def entries(a): return a.T.reshape(-1)
def pack(v, P): return np.ascontiguousarray(np.asarray(v, np.int32).reshape(-1, P).T)
def split(rng, total, parts):
    c = np.sort(rng.integers(0, total + 1, parts - 1)); return np.diff(np.concatenate([[0], c, [total]]))
def lists(rng, how):
    s = np.concatenate([[0], rng.integers(1 - Q // 2, Q // 2 + 1, N - 1), [int(rng.integers(1 - Q // 2, 1))]])
    if how == "early": s[1:] = -Q; s[N] = -2 * Q
    if how == "late": s[1:] = Q; s[N] = 0
    if how == "long":
        z = int(rng.integers(1, N - 1)); s[1:z] = -rng.integers(1, Q, z - 1); s[z] = -Q; s[z + 1] = Q; s[z + 2:N] = rng.integers(1, Q, N - z - 2); s[N] = -int(rng.integers(0, Q - s[N - 1] + 1))
    if how == "sway":
        z = int(rng.integers(1, N - 2)); e = int(rng.integers(z + 1, N - 1)); s[1:] = -rng.integers(Q // 2 + 1, Q, N); s[z + 1:e + 1] = rng.integers(Q // 2 + 1, Q - 1, e - z); s[e + 1] = s[e] - Q; s[N] = s[N - 1] - Q + int(rng.integers(1, -s[N - 1]))
    tot = Q + np.diff(s)
    L = np.stack([split(rng, int(t), J) for t in tot])
    if how == "gaps":
        L = np.zeros((N, J), np.int64)
        for r in range(N): m = 1 if r & 1 else 8; L[r, 1 + rng.permutation(J - 2)[:m]] = split(rng, int(tot[r]), m)
    if how == "long":
        L = np.zeros((N, J), np.int64); L[np.arange(N), rng.integers(0, J, N)] = tot
    return {"ln": np.stack([pack(l, 16) for l in L])}
def setup_inputs(rng):
    return dict({"x": rng.standard_normal((N, 128, J), dtype=np.float32)}, **lists(rng, "uniform"))
def setup_inputs_early(rng):
    d = setup_inputs(rng); d.update(lists(rng, "early"))
    for k in ("x",): d[k] = (d[k].astype(np.float32) * 1048576.0).astype(d[k].dtype)
    return d
def setup_inputs_gaps(rng):
    d = setup_inputs(rng); d.update(lists(rng, "gaps"))
    for k in ("x",): d[k] = (d[k].astype(np.float32) * (1 / 1024.0)).astype(d[k].dtype)
    return d
def setup_inputs_late(rng):
    d = setup_inputs(rng); d.update(lists(rng, "late"))
    return d
def setup_inputs_long(rng):
    d = setup_inputs(rng); d.update(lists(rng, "long"))
    return d
def setup_inputs_sway(rng):
    d = setup_inputs(rng); d.update(lists(rng, "sway"))
    return d
def check_inputs(x):
    bad = []
    if x["ln"].min() < 0 or x["ln"].max() >= N * Q + 1: bad.append("ln out of range")
    if int(x["ln"].sum()) > N * Q: bad.append("the lengths come to more than N * Q")
    c = np.concatenate([[0], np.cumsum([int(a.sum()) for a in x["ln"]])])
    if any(c[r] < (r - 1) * Q or c[r + 1] > (r + 2) * Q for r in range(N)): bad.append("the sums of the lengths before or up to a rank leave their bounds")
    return bad
def reference(x, ln):
    got = np.concatenate([np.repeat(x[r], entries(ln[r]), axis=1) for r in range(N)], axis=1)[:, :N * Q]
    Y = np.zeros((128, N * Q), x.dtype); Y[:, :got.shape[1]] = got
    return {"y": np.stack([Y[:, Q * r:Q * r + Q] for r in range(N)])}

from concourse.bass import DstId, RemoteDMATransfer
from concourse.mybir import AluOpType, ActivationFunctionType

N, J, Q = 8, 256, 1024
BIG = 201326592.0
ZC = 3 * J
WW = ZC + 4

SCRATCH = {
    "lst": ("sbuf", [128, 2 * N], "int32"),
    "win": ("sbuf", [128, WW], "float32"),
    "yb": ("sbuf", [128, Q], "float32"),
    "ones": ("sbuf", [128, 128], "float32"),
    "key": ("sbuf", [128, 128], "float32"),
    "msame": ("sbuf", [128, 128], "float32"),
    "mle": ("sbuf", [128, 128], "float32"),
    "mlt": ("sbuf", [128, 128], "float32"),
    "pc": ("sbuf", [128, 4], "int32"),
    "kc": ("sbuf", [128, 4], "float32"),
    "cst": ("sbuf", [128, 6], "float32"),
    "r6": ("sbuf", [128, 6], "float32"),
    "of": ("sbuf", [128, 2], "float32"),
    "nf": ("sbuf", [128, 4], "float32"),
    "ef": ("sbuf", [128, 2 * N], "float32"),
    "lf": ("sbuf", [128, 4], "float32"),
    "hi": ("sbuf", [128, 6], "float32"),
    "lo": ("sbuf", [128, 6], "float32"),
    "c16": ("sbuf", [128, 64], "bfloat16"),
    "bt": ("sbuf", [128, 128], "bfloat16"),
    "nh": ("sbuf", [128, 128], "bfloat16"),
    "sg": ("sbuf", [128, 384], "bfloat16"),
    "eq": ("sbuf", [128, 384], "bfloat16"),
    "u": ("sbuf", [128, 768], "bfloat16"),
    "off": ("sbuf", [128, 64], "uint16"),
    "F": ("psum", [128, 512], "float32"),
    "I": ("psum", [128, 512], "float32"),
}
SEMAPHORES = (["h%d" % s for s in range(N)] + ["q%d" % s for s in range(N)] +
              ["xl", "xr", "ls", "sln", "sx", "st", "dv", "ac", "pe", "gp"])


def plan(cores, topo):
    n = len(cores)
    def onchip(a, b):
        return topo.host(cores[a]) == topo.host(cores[b]) and topo.chip(cores[a]) == topo.chip(cores[b])
    def may(a, b):
        return topo.may_write(cores[a], cores[b])
    nb = [[m for m in (r - 1, r + 1) if 0 <= m < n] for r in range(n)]
    base = [list(range(0, max(0, r - 1))) for r in range(n)]
    relay = {}
    for d in range(n):
        for s in base[d]:
            if not may(s, d):
                c = [m for m in range(n) if m not in (s, d) and may(s, m) and may(m, d)]
                c.sort(key=lambda m: (sum(not onchip(m, k) for k in nb[m]), m))
                relay[(s, d)] = c[0]
    direct = set((s, d) for d in range(n) for s in nb[d] + base[d] if (s, d) not in relay)
    for (s, d), m in relay.items():
        if s != m:
            direct.add((s, m))
    feed = set((s, m) for (s, d), m in relay.items())
    for d in range(n):
        for s in base[d]:
            if (s, d) in direct and (s, d) not in feed:
                for m in range(d):
                    if onchip(m, d) and (s, m) in direct:
                        relay[(s, d)] = m
                        direct.discard((s, d))
    wave1 = [sorted([d for d in range(n) if (s, d) in direct],
                    key=lambda d: ((s, d) not in feed, d not in nb[s], d)) for s in range(n)]
    wave2 = {}
    for (s, d), m in sorted(relay.items()):
        first = s - s % 2
        if s == first:
            for e in wave2.setdefault(m, []):
                if e[0] == first:
                    e[1].append(d)
                    break
            else:
                wave2[m].append((first, [d]))
    return nb, base, relay, wave1, wave2, onchip


def rank_program(g, core, T, topo):
    r = T.rank_of(core)
    if r is None:
        return
    cores = T.cores
    nb, base, relay, wave1, wave2, onchip = plan(cores, topo)
    n = len(cores)
    A = AluOpType
    AF = ActivationFunctionType

    def masks(a):
        chip_mask = max(topo.mask(cores[a], cores[d]) for d in range(n) if d != a and onchip(a, d))
        off_mask = max(topo.mask(cores[a], cores[d]) for d in range(n) if not onchip(a, d) and topo.may_write(cores[a], cores[d]))
        return chip_mask & ~off_mask, off_mask

    def count(a, d):
        on, off = masks(a)
        return bin(on if onchip(a, d) else off).count("1")

    on_mask, off_mask = masks(r)
    total = {}

    def dst(d):
        rid, pid = topo.addr(cores[d], core)
        return DstId(rid=rid, pnc=pid)

    def send(groups):
        tr = []
        for ds, src, places, sem in groups:
            m = on_mask if onchip(r, ds[0]) else off_mask
            tr.append(RemoteDMATransfer(dst_ids=[dst(d) for d in ds], dma_engine_mask=m, remote_sem=T.sem[sem], srcs=[src], dsts=places))
            total["ls"] = total.get("ls", 0) + bin(m).count("1")
        g.remote_dma_fused(tr, local_sem=T.sem["ls"])

    def split(ds):
        return [x for x in ([d for d in ds if not onchip(r, d)], [d for d in ds if onchip(r, d)]) if x]

    cnt = {"dv": 0, "ac": 0, "pe": 0, "gp": 0}

    def inc(ins, s):
        cnt[s] += 1
        ins.then_inc(T.sem[s], 1)
        return cnt[s]

    def arrive(q, s):
        v = count(s, r)
        total["h%d" % s] = v
        q.wait_ge(T.sem["h%d" % s], v)

    V, S, P = g.vector, g.scalar, g.tensor

    own = T.lst[:, 2 * r:2 * r + 2]
    g.sync.dma_start(own, T.ln[:, :]).then_inc(T.sem["sln"], 16)
    total["sln"] = 16
    S.dma_start(T.win[:, J:2 * J], T.x[:, :]).then_inc(T.sem["sx"], 16)
    total["sx"] = 16

    inc(g.iota(T.pc[:, 0:1], [[0, 1]], 0, 1), "gp")
    gp_key = inc(g.iota(T.key[:, :], [[1, 16], [16, 8]], 0, 0, allow_small_or_imprecise_dtypes=True), "gp")
    g.wait_ge(T.sem["sln"], 16)
    send([(ds, own, [own] * len(ds), "h%d" % r) for ds in split(wave1[r])])
    g.wait_ge(T.sem["sx"], 16)
    gr = []
    for d in sorted(nb[r], key=lambda d: onchip(r, d)):
        place = T.win[:, 0:J] if d > r else T.win[:, 2 * J:3 * J]
        gr.append(([d], T.win[:, J:2 * J], [place], "xl" if d > r else "xr"))
    send(gr)
    inc(g.iota(T.c16[:, :], [[16, 64]], 0, 0, allow_small_or_imprecise_dtypes=True), "gp")
    gp_bt = inc(g.iota(T.bt[:, :], [[0, 8], [1, 16]], -8, 0, allow_small_or_imprecise_dtypes=True), "gp")
    for first, ds in wave2.get(r, []):
        for s in (first, first + 1):
            if s != r:
                arrive(g, s)
        pair = T.lst[:, 2 * first:2 * first + 4]
        send([(dd, pair, [pair] * len(dd), "q%d" % first) for dd in split(ds)])

    def v(ins):
        return inc(ins, "dv")

    def vdep():
        V.wait_ge(T.sem["dv"], cnt["dv"])

    v(V.memset(T.cst[:, :], (-float(Q) * r - 8.0) / 128.0))
    dv_ones = v(V.memset(T.ones[:, :], 1.0))
    v(V.memset(T.r6[:, :], 0.0))
    v(V.memset(T.nh[:, :], -0.5))
    V.wait_ge(T.sem["gp"], gp_key)
    v(V.tensor_scalar(T.pc[:, 1:2], T.pc[:, 0:1], 7, None, A.bitwise_and))
    v(V.tensor_scalar(T.pc[:, 2:3], T.pc[:, 0:1], 3, None, A.arith_shift_right))
    vdep()
    v(V.tensor_scalar(T.kc[:, 0:1], T.pc[:, 1:2], 16.0, None, A.mult))
    v(V.tensor_scalar(T.kc[:, 1:2], T.pc[:, 1:2], 16.0, 16.0, A.mult, A.add))
    vdep()
    v(V.tensor_tensor(T.kc[:, 2:3], T.kc[:, 0:1], T.pc[:, 2:3], A.add))
    vdep()
    v(V.tensor_scalar(T.msame[:, :], T.key[:, :], T.kc[:, 2:3], None, A.is_ge))
    v(V.tensor_scalar(T.mlt[:, :], T.key[:, :], T.kc[:, 1:2], None, A.is_ge))
    dv_m = v(V.tensor_scalar(T.mle[:, :], T.key[:, :], T.kc[:, 0:1], None, A.is_ge))
    if r == 0:
        v(V.memset(T.win[:, 0:J], 0.0))
    v(V.memset(T.win[:, (ZC if r + 1 < n else 2 * J):WW], 0.0))

    P.wait_ge(T.sem["dv"], dv_ones)
    inc(P.matmul(T.F[:, 0:6], T.ones[:, :], T.cst[:, :], True, False), "pe")

    def prefix(src, a, b, need):
        P.wait_ge(T.sem["dv"], need)
        w = b - a
        inc(P.matmul(T.F[:, a:b], T.msame[:, :], src[:, 0:w], False, False), "pe")
        for k in range(0, w, 2):
            inc(P.matmul(T.F[:, a + k:a + k + 1], T.mlt[:, :], src[:, k + 1:k + 2], False, False), "pe")
            inc(P.matmul(T.F[:, a + k + 1:a + k + 2], T.mle[:, :], src[:, k:k + 1], False, False), "pe")

    def addto(b, src, k):
        vdep()
        v(V.tensor_scalar(T.r6[:, b[0]:b[1]], T.r6[:, b[0]:b[1]], src[:, k:k + 1], src[:, k + 1:k + 2], A.add, A.add))

    V.wait_ge(T.sem["sln"], 16)
    k = v(V.tensor_copy(T.of[:, :], own))
    prefix(T.of, 0, 2, k)
    addto((2, 4), T.of, 0)
    nxt, prv = r + 1 < n, r > 0
    order = ([("n", r + 1)] if nxt else []) + ([("p", r - 1)] if prv else [])
    for tag, s in order:
        arrive(V, s)
        c = 0 if tag == "n" else 2
        k = v(V.tensor_copy(T.nf[:, c:c + 2], T.lst[:, 2 * s:2 * s + 2]))
    lo_c, hi_c = (0 if nxt else 2), (4 if prv else 2)
    prefix(T.nf[:, lo_c:hi_c] if False else T.nf, 2, 6, k) if (nxt and prv) else None
    if not (nxt and prv):
        P.wait_ge(T.sem["dv"], k)
        c = 0 if nxt else 2
        inc(P.matmul(T.F[:, 2 + c:4 + c], T.msame[:, :], T.nf[:, c:c + 2], False, False), "pe")
        inc(P.matmul(T.F[:, 2 + c:3 + c], T.mlt[:, :], T.nf[:, c + 1:c + 2], False, False), "pe")
        inc(P.matmul(T.F[:, 3 + c:4 + c], T.mle[:, :], T.nf[:, c:c + 1], False, False), "pe")
    if prv:
        addto((0, 4), T.nf, 2)
    early = [s for s in base[r] if (s, r) not in relay]
    late = sorted(set(s - s % 2 for s in base[r] if (s, r) in relay))
    for s in early:
        arrive(V, s)
        v(V.tensor_copy(T.ef[:, 2 * s:2 * s + 2], T.lst[:, 2 * s:2 * s + 2]))
        addto((0, 6), T.ef, 2 * s)
    for first in late:
        m = relay[(first, r)]
        total["q%d" % first] = count(m, r)
        V.wait_ge(T.sem["q%d" % first], count(m, r))
    if late:
        a = T.lst[:, 2 * late[0]:2 * late[0] + 4]
        if len(late) == 1:
            v(V.tensor_tensor(T.lf[:, 0:2], T.lst[:, 2 * late[0]:2 * late[0] + 2], T.lst[:, 2 * late[0] + 2:2 * late[0] + 4], A.add))
            addto((0, 6), T.lf, 0)
        else:
            v(V.tensor_tensor(T.lf[:, 0:4], a, T.lst[:, 2 * late[1]:2 * late[1] + 4], A.add))
            addto((0, 6), T.lf, 0)
            addto((0, 6), T.lf, 2)
    P.wait_ge(T.sem["dv"], cnt["dv"])
    pe_F = inc(P.matmul(T.F[:, 0:6], T.ones[:, :], T.r6[:, :], False, True), "pe")

    V.wait_ge(T.sem["pe"], pe_F)
    dv_hi = v(V.tensor_scalar(T.hi[:, :], T.F[:, 0:6], BIG, BIG, A.add, A.subtract))
    vdep()
    v(V.tensor_tensor(T.lo[:, :], T.F[:, 0:6], T.hi[:, :], A.subtract))
    V.wait_ge(T.sem["gp"], gp_bt)
    S.wait_ge(T.sem["gp"], gp_bt)
    S.wait_ge(T.sem["dv"], dv_hi)
    for k in range(6):
        e, w = slice(64 * k, 64 * k + 64), slice(128 * k, 128 * k + 128)
        v(V.tensor_scalar(T.eq[:, e], T.c16[:, :], T.hi[:, k:k + 1], None, A.is_equal))
        if k == 0:
            V.wait_ge(T.sem["dv"], cnt["dv"] - 1)
        dk = v(V.tensor_scalar(T.u[:, w], T.bt[:, :], T.lo[:, k:k + 1], 0.5, A.is_ge, A.subtract))
        ak = inc(S.activation(T.sg[:, e], T.c16[:, :], AF.Sign, bias=T.hi[:, k:k + 1], scale=-1.0), "ac")
        P.wait_ge(T.sem["ac"], ak)
        inc(P.matmul(T.I[:, 0:64], T.nh[:, :], T.sg[:, e], k == 0, False), "pe")
        P.wait_ge(T.sem["dv"], dk)
        pe_I = inc(P.matmul(T.I[:, 0:64], T.u[:, w], T.eq[:, e], False, k == 5), "pe")
    V.wait_ge(T.sem["pe"], pe_I)
    dv_off = v(V.tensor_scalar(T.off[:, :], T.I[:, 0:64], 384.0, None, A.add))

    for q in (V, S):
        q.wait_ge(T.sem["sx"], 16)
        if prv:
            total["xl"] = count(r - 1, r)
            q.wait_ge(T.sem["xl"], total["xl"])
        if nxt:
            total["xr"] = count(r + 1, r)
            q.wait_ge(T.sem["xr"], total["xr"])
        q.wait_ge(T.sem["dv"], dv_off)
    window = T.win[:, :]
    B = 256
    done = {}
    for i in (0, 1):
        q0 = i * B
        done[i] = v(V.tensor_copy(T.yb[:, q0:q0 + B], window.indirect(T.off[:, q0 // 16:(q0 + B) // 16])))
        q0 = (2 + i) * B
        done[2 + i] = inc(S.activation(T.yb[:, q0:q0 + B], window.indirect(T.off[:, q0 // 16:(q0 + B) // 16]), AF.Copy, bias=-0.0), "ac")
    for i, q, s in ((0, g.sync, "dv"), (2, g.sync, "ac"), (1, g.sync, "dv"), (3, S, "ac")):
        q.wait_ge(T.sem[s], done[i])
        q.dma_start(T.y[:, i * B:(i + 1) * B], T.yb[:, i * B:(i + 1) * B]).then_inc(T.sem["st"], 16)
    total["st"] = 64

    for s, k in list(total.items()) + [x for x in cnt.items() if x[1]]:
        g.wait_ge(T.sem[s], k)
